import numpy as np
import ml_dtypes


def mxq(x, axis, fmt="e4m3"):
    dtype, down = {"e4m3": (ml_dtypes.float8_e4m3fn, 7), "e5m2": (ml_dtypes.float8_e5m2, 14)}[fmt]
    v = np.moveaxis(np.asarray(x, np.float32).astype(ml_dtypes.bfloat16).astype(np.float64), axis, -1)
    blocks = v.reshape(v.shape[:-1] + (-1, 32))
    amax = np.abs(blocks).max(-1, keepdims=True)
    byte = np.maximum(np.where(amax > 0, np.frexp(amax)[1] - 1 + 127, 0) - down, 1)
    scale = np.exp2(byte - 127.0)
    codes = (blocks / scale).astype(np.float32).astype(dtype).astype(np.float64)
    return np.moveaxis((codes * scale).reshape(v.shape), -1, axis)


WIDE = False


def mx_kscale(k):
    if not WIDE:
        return np.ones(k)
    levels = np.array([24, -24, 12, -12, 0])
    if k % 512:
        return np.exp2(np.random.permutation(np.resize(levels, k // 32))).repeat(32)
    a = np.empty((k // 512, 16))
    for p in range(k // 512):
        a[p, :8] = np.random.permutation(np.resize(levels, 8))
        for g in range(8):
            far = levels[np.abs(levels - a[p, g]) >= 10]
            a[p, g + 8] = far[np.random.randint(len(far))]
    return np.exp2(a.ravel()).repeat(32)


def f64(x):
    return np.asarray(x).astype(np.float64)


def striped(idx):
    return np.tile(idx.reshape(-1, 16).T, (8, 1)).astype(np.uint16)


def unstriped(offs):
    return offs[:16].T.reshape(-1).astype(np.int64)


E2M1 = np.array([0.0, 0.5, 1.0, 1.5, 2.0, 3.0, 4.0, 6.0, -0.0, -0.5, -1.0, -1.5, -2.0, -3.0, -4.0, -6.0])


def pack_weight(w, fmt):
    k, n = w.shape
    w = f64(np.asarray(w, np.float32).astype(ml_dtypes.bfloat16)).reshape(k // 32, 32, n)
    amax = np.abs(w).max(1)
    if fmt == "e4m3":
        byte = np.frexp(amax)[1] - 1 + 127 - 7
    else:
        mant, ex = np.frexp(amax / 6.0)
        byte = np.where(mant > 0.5, ex, ex - 1) + 127
    byte = np.clip(np.where(amax > 0, byte, 1), 1, 254)
    scaled = (w * np.exp2(127.0 - byte)[:, None, :]).reshape(k, n).astype(np.float32)
    by_word = np.ascontiguousarray(scaled.reshape(k // 512, 128, 4, n).transpose(0, 1, 3, 2))
    if fmt == "e4m3":
        words = by_word.astype(ml_dtypes.float8_e4m3fn).view(np.uint8)
    else:
        c = by_word.astype(ml_dtypes.float4_e2m1fn).view(np.uint8) & 0xF
        words = (c[..., 0::2] | (c[..., 1::2] << 4)).reshape(k // 512, 128, 2 * n)
    return np.ascontiguousarray(words), np.ascontiguousarray(byte.astype(np.uint8).reshape(k // 512, 16, n))


def unpack_weight(words, scales, fmt):
    g, _, n = scales.shape
    words = np.ascontiguousarray(words).reshape(g, 128, n, -1)
    if fmt == "e4m3":
        vals = words.view(ml_dtypes.float8_e4m3fn).astype(np.float64)
    else:
        nib = np.empty((g, 128, n, 4), np.uint8)
        nib[..., 0::2] = words & 0xF
        nib[..., 1::2] = words >> 4
        vals = E2M1[nib]
    vals = vals * np.repeat(np.exp2(scales.astype(np.float64) - 127.0), 8, axis=1)[..., None]
    return vals.transpose(0, 1, 3, 2).reshape(g * 512, n)


def pack_table4(v):
    words, scales = pack_weight(v, "e2m1")
    g, t = words.shape[0] // 2, v.shape[1]
    return np.ascontiguousarray(words.reshape(g, 2, 128, t, 2).transpose(0, 2, 3, 1, 4).reshape(g, 128, t, 4)), scales


def unpack_table4(words, scales):
    g, _, t, _ = words.shape
    return unpack_weight(words.reshape(g, 128, t, 2, 2).transpose(0, 3, 1, 2, 4).reshape(2 * g, 128, 2 * t), scales, "e2m1")


def silu(f):
    return f / (1.0 + np.exp(-np.maximum(f, -700.0)))


def sigm(f):
    return 1.0 / (1.0 + np.exp(-np.maximum(f, -700.0)))


K, N, T, J = 1024, 512, 2048, 1024


def setup_inputs():
    n = np.random.standard_normal
    s = mx_kscale(K)[:, None]
    p_tab = pack_table4(n((K, T)) * s)
    p_wa = pack_weight(n((K, N)) / np.sqrt(2 * K) / s, "e2m1")
    p_wb = pack_weight(n((K, N)) / np.sqrt(2 * K) / s, "e2m1")
    p_wo = pack_weight(n((K, N)) / np.sqrt(K) / s, "e2m1")
    return {
        "tab_words": p_tab[0],
        "tab_scales": p_tab[1],
        "wa_words": p_wa[0],
        "wa_scales": p_wa[1],
        "wb_words": p_wb[0],
        "wb_scales": p_wb[1],
        "wc": (n((K, N)) / np.sqrt(K) / s).astype(np.float32),
        "wo_words": p_wo[0],
        "wo_scales": p_wo[1],
        "b": (0.3 * n(N)).astype(np.float32),
        "wgo": np.tile(np.random.uniform(0.5, 2.0, J), (128, 1)).astype(np.float32),
        "offs": striped(np.random.permutation(T)[:J]),
        "offs2": striped(np.random.permutation(T)[:J]),
    }


def reference(tab_words, tab_scales, wa_words, wa_scales, wb_words, wb_scales, wc, wo_words, wo_scales, b, wgo, offs, offs2):
    idx = unstriped(offs)
    idx2 = unstriped(offs2)
    tab_ = unpack_table4(tab_words, tab_scales)[:, idx]
    tabb_ = unpack_table4(tab_words, tab_scales)[:, idx2]
    wa_ = unpack_weight(wa_words, wa_scales, "e2m1")
    wb_ = unpack_weight(wb_words, wb_scales, "e2m1")
    za = wa_.T @ tabb_ + wb_.T @ tab_
    eta = sigm(za)
    wc_ = mxq(f64(wc), 0, "e4m3")
    ms = wc_.T @ tab_
    wo_ = unpack_weight(wo_words, wo_scales, "e2m1")
    ow = wo_.T @ tabb_
    out = np.zeros((N, T))
    out[:, idx2] = f64(wgo)[0] * (silu(ow + eta * ms + f64(b)[:, None]))
    return out

@@ -1,0 +1,197 @@
+from contextlib import ExitStack
+
+import concourse.mybir as mybir
+
+K, N, T, J = 1024, 512, 2048, 1024
+FLOPS = 4 * 2 * K * N * J
+
+F32 = mybir.dt.float32
+BF16 = mybir.dt.bfloat16
+I32 = mybir.dt.int32
+U32 = mybir.dt.uint32
+U16 = mybir.dt.uint16
+U8 = mybir.dt.uint8
+FP8X4 = mybir.dt.float8_e4m3fn_x4
+FP4X4 = mybir.dt.float4_e2m1fn_x4
+ALU = mybir.AluOpType
+ACT = mybir.ActivationFunctionType
+
+P = 128
+PASSES = 2
+CH = 512
+CHUNKS = J // CH
+NT = N // P
+HALF = 256
+SRC, TGT = 0, 1
+
+
+def tile_list_rgg_ownsilu_kernel(
+    tc, tab_words, tab_scales, wa_words, wa_scales, wb_words, wb_scales, wc, wo_words, wo_scales, b, wgo, offs, offs2, out
+):
+    nc = tc.nc
+    with ExitStack() as ctx:
+        keep = ctx.enter_context(tc.tile_pool(name="keep", bufs=1))
+        ring = ctx.enter_context(tc.tile_pool(name="ring", bufs=3))
+        stage = ctx.enter_context(tc.tile_pool(name="stage", bufs=1))
+        psum = ctx.enter_context(tc.psum_pool(name="psum", bufs=2))
+
+        lists = [keep.tile([P, J // 16], U16, name="list_src"), keep.tile([P, J // 16], U16, name="list_tgt")]
+        words = keep.tile([P, T], I32, name="words", align_bytes=64)
+        scale_win = keep.tile([P, T // 4], I32, name="scale_win", align_bytes=64)
+        w_scale = keep.tile([P, 3, PASSES, N // 4], I32, name="w_scale", align_bytes=64)
+        g_scale = [keep.tile([P, 2, CH // 4], I32, name="g_scale%d" % c, align_bytes=64) for c in range(CHUNKS)]
+        s_scale = [keep.tile([P, 2, CH // 4], I32, name="s_scale%d" % c, align_bytes=64) for c in range(CHUNKS)]
+        g_words = [[keep.tile([P, CH], U32, name="g_words%d%d" % (c, l), align_bytes=64) for l in range(2)] for c in range(CHUNKS)]
+        parted = [[keep.tile([P, PASSES, 2 * CH], U8, name="parted%d%d" % (c, l), align_bytes=64) for l in range(2)] for c in range(CHUNKS)]
+        wc_grp = [keep.tile([P, PASSES, HALF, 4], BF16, name="wc_grp%d" % h, align_bytes=64) for h in range(2)]
+        wc_codes = [keep.tile([P, PASSES, HALF], U32, name="wc_codes%d" % h, align_bytes=64) for h in range(2)]
+        wc_scale = [keep.tile([P, PASSES, HALF], U8, name="wc_scale%d" % h, align_bytes=64) for h in range(2)]
+        bias = keep.tile([P, NT], F32, name="bias")
+        rows = [keep.tile([P, T], F32, name="rows%d" % i) for i in range(2)]
+        warm = stage.tile([P, 8], F32, name="late_f", align_bytes=64)
+        warm_out = stage.tile([P, 8], F32, name="late_w", align_bytes=64)
+
+        nc.vector.memset(scale_win[:], 0)
+        nc.vector.memset(warm[:], 0.0)
+        nc.vector.memset(w_scale[:], 0)
+        for c in range(CHUNKS):
+            nc.vector.memset(s_scale[c][:], 0)
+        nc.scalar.activation(warm_out[:], warm[:], ACT.Silu)
+        late_f = stage.tile([P, 2, J], F32, name="late_f", align_bytes=64)
+        late_w = stage.tile([P, 3, PASSES, N // 2], I32, name="late_w", align_bytes=64)
+        slot = [late_f[:, s, :] for s in range(2)]
+        w_words = [late_w[:, i, :, :] for i in range(3)]
+        wc_slot = {(0, 0): 0, (0, 1): 1, (1, 0): 0, (1, 1): 0}
+        edge_w = slot[1]
+
+        nc.sync.dma_start(lists[TGT][:], offs2)
+        nc.sync.dma_start(lists[SRC][:], offs)
+        for q in range(4):
+            nc.sync.dma_start(scale_win[32 * q : 32 * q + 8, :], tab_scales[:, 4 * q : 4 * q + 4, :].bitcast(I32))
+        nc.sync.dma_start(words[:], tab_words[0].rearrange("p t b -> p (t b)").bitcast(I32))
+
+        def load_scales(i, scales, queue):
+            for q in range(4):
+                queue.dma_start(
+                    w_scale[32 * q : 32 * q + 4, i, :, :],
+                    scales[:, 4 * q : 4 * q + 4, :].rearrange("a r n -> r a n").bitcast(I32),
+                )
+
+        def load_words(i, w):
+            nc.sync.dma_start(w_words[i], w.rearrange("a p n -> p a n").bitcast(I32))
+
+        def load_wc(h, a):
+            nc.sync.dma_start(
+                slot[wc_slot[h, a]].rearrange("p (i n) -> p i n", i=4),
+                wc[512 * a : 512 * (a + 1), HALF * h : HALF * (h + 1)].rearrange("(p i) n -> p i n", i=4),
+            )
+
+        load_wc(0, 0)
+        load_words(0, wa_words)
+        load_words(1, wb_words)
+        load_wc(0, 1)
+        load_scales(0, wa_scales, nc.sync)
+        load_scales(1, wb_scales, nc.sync)
+        load_words(2, wo_words)
+        load_scales(2, wo_scales, nc.gpsimd)
+        with nc.allow_non_contiguous_dma("one bias value a partition"):
+            nc.gpsimd.dma_start(bias[:], b.rearrange("(t p) -> p t", p=P))
+        for i in range(2):
+            nc.gpsimd.memset(rows[i][:], 0.0)
+
+        def piece(l, c):
+            return lists[l][:, c * (CH // 16) : (c + 1) * (CH // 16)]
+
+        def gather_scales(c):
+            for l in (TGT, SRC):
+                nc.vector.tensor_copy(g_scale[c][:, l, :].bitcast(U8), scale_win[:].bitcast(U8).indirect(piece(l, c)))
+            nc.sync.dma_start(s_scale[c][0:112, :, :], g_scale[c][4:116, :, :])
+
+        def gather_words(c):
+            for l in (TGT, SRC):
+                nc.vector.tensor_copy(g_words[c][l][:], words[:].bitcast(U32).indirect(piece(l, c)))
+            for l in (TGT, SRC):
+                nc.vector.tensor_copy(
+                    parted[c][l][:].bitcast(U16),
+                    g_words[c][l][:].bitcast(U16).rearrange("p (j d) -> p d j", d=2),
+                )
+
+        def group_wc(h, a):
+            nc.scalar.copy(wc_grp[h][:, a, :, :], slot[wc_slot[h, a]].rearrange("p (i n) -> p n i", i=4))
+
+        def quantize_wc(h):
+            nc.vector.quantize_mx(
+                out=wc_codes[h][:].rearrange("p a n -> p (a n)").bitcast(FP8X4),
+                scales=wc_scale[h][:].rearrange("p a n -> p (a n)"),
+                in_=wc_grp[h][:].rearrange("p a n i -> p (a n i)"),
+            )
+
+        def table(c, l, a):
+            plane = g_scale[c] if a == 0 else s_scale[c]
+            return parted[c][l][:, a, :].bitcast(FP4X4), plane[:, l, :].bitcast(U8)
+
+        def packed_weight(i, a, nt):
+            return (
+                w_words[i][:, a, 64 * nt : 64 * (nt + 1)].bitcast(FP4X4),
+                w_scale[:, i, a, 32 * nt : 32 * (nt + 1)].bitcast(U8),
+            )
+
+        def wc_weight(a, nt):
+            h, o = divmod(nt * P, HALF)
+            return wc_codes[h][:, a, o : o + P].bitcast(FP8X4), wc_scale[h][:, a, o : o + P]
+
+        def product(acc, pairs):
+            for i, ((w, ws), (v, vs)) in enumerate(pairs):
+                nc.tensor.matmul_mx(
+                    out=acc[:], lhsT=w, lhsT_scale=ws, rhs=v, rhs_scale=vs, start=(i == 0), stop=(i == len(pairs) - 1)
+                )
+
+        def front(nt, c, first=False):
+            za = psum.tile([P, CH], F32, name="za")
+            ms = psum.tile([P, CH], F32, name="ms", bufs=3)
+            ow = psum.tile([P, CH], F32, name="ow", bufs=3)
+            product(za, [(packed_weight(i, a, nt), table(c, l, a)) for a in range(PASSES) for i, l in ((0, TGT), (1, SRC))])
+            product(ms, [(wc_weight(a, nt), table(c, SRC, a)) for a in range(PASSES)])
+            product(ow, [(packed_weight(2, a, nt), table(c, TGT, a)) for a in range(PASSES)])
+            th = ring.tile([P, CH], F32, name="th")
+            nc.scalar.activation(th[:], za[:], ACT.Tanh, scale=0.5)
+            msg = ring.tile([P, CH], F32, name="msg")
+            nc.vector.scalar_tensor_tensor(msg[:], th[:], 1.0, ms[:], ALU.add, ALU.mult)
+            both = ring.tile([P, CH], F32, name="both")
+            if first:
+                nc.vector.scalar_tensor_tensor(both[:], ow[:], 2.0, msg[:], ALU.mult, ALU.add)
+            else:
+                own = ring.tile([P, CH], F32, name="own")
+                nc.scalar.activation(own[:], ow[:], ACT.Copy, scale=2.0)
+                nc.gpsimd.tensor_tensor(both[:], msg[:], own[:], ALU.add)
+            act = ring.tile([P, CH], F32, name="act")
+            nc.scalar.activation(act[:], both[:], ACT.Silu, bias=bias[:, nt : nt + 1], scale=0.5)
+            val = ring.tile([P, CH], F32, name="val", bufs=4)
+            (nc.vector if first else nc.gpsimd).tensor_tensor(val[:], act[:], edge_w[:, c * CH : (c + 1) * CH], ALU.mult)
+            return val
+
+        def back(nt, c, val):
+            nc.vector.tensor_copy(rows[nt % 2][:].indirect(piece(TGT, c)), val[:])
+            if c == CHUNKS - 1:
+                nc.sync.dma_start(out[nt * P : (nt + 1) * P, :], rows[nt % 2][:])
+
+        gather_scales(0)
+        gather_words(0)
+        group_wc(0, 0)
+        group_wc(0, 1)
+        gather_scales(1)
+        quantize_wc(0)
+        load_wc(1, 0)
+        nc.sync.dma_start(edge_w, wgo)
+        group_wc(1, 0)
+        load_wc(1, 1)
+        group_wc(1, 1)
+        units = [(nt, c) for nt in range(NT) for c in range(CHUNKS)]
+        vals = {0: front(*units[0], first=True)}
+        gather_words(1)
+        vals[1] = front(*units[1])
+        quantize_wc(1)
+        for u in range(len(units)):
+            if u + 2 < len(units):
+                vals[u + 2] = front(*units[u + 2])
+            back(*units[u], vals[u])

@@ -32,43 +32,35 @@ def tile_list_rgg_ownsilu_kernel(
     with ExitStack() as ctx:
         keep = ctx.enter_context(tc.tile_pool(name="keep", bufs=1))
         ring = ctx.enter_context(tc.tile_pool(name="ring", bufs=3))
-        stage = ctx.enter_context(tc.tile_pool(name="stage", bufs=1))
         psum = ctx.enter_context(tc.psum_pool(name="psum", bufs=2))
 
         lists = [keep.tile([P, J // 16], U16, name="list_src"), keep.tile([P, J // 16], U16, name="list_tgt")]
         words = keep.tile([P, T], I32, name="words", align_bytes=64)
         scale_win = keep.tile([P, T // 4], I32, name="scale_win", align_bytes=64)
         w_scale = keep.tile([P, 3, PASSES, N // 4], I32, name="w_scale", align_bytes=64)
-        g_scale = [keep.tile([P, 2, CH // 4], I32, name="g_scale%d" % c, align_bytes=64) for c in range(CHUNKS)]
+        w_words = [keep.tile([P, PASSES, N // 2], I32, name="w_words%d" % i, align_bytes=64) for i in range(3)]
+        g_scale = {0: keep.tile([P, 2, CH // 4], I32, name="g_scale0", align_bytes=64)}
         s_scale = [keep.tile([P, 2, CH // 4], I32, name="s_scale%d" % c, align_bytes=64) for c in range(CHUNKS)]
-        g_words = [[keep.tile([P, CH], U32, name="g_words%d%d" % (c, l), align_bytes=64) for l in range(2)] for c in range(CHUNKS)]
+        g_words = {(0, l): keep.tile([P, CH], U32, name="g_words0%d" % l, align_bytes=64) for l in range(2)}
         parted = [[keep.tile([P, PASSES, 2 * CH], U8, name="parted%d%d" % (c, l), align_bytes=64) for l in range(2)] for c in range(CHUNKS)]
+        wc_raw = [keep.tile([P, PASSES, 4 * HALF], F32, name="wc_raw%d" % h, align_bytes=64) for h in range(2)]
         wc_grp = [keep.tile([P, PASSES, HALF, 4], BF16, name="wc_grp%d" % h, align_bytes=64) for h in range(2)]
         wc_codes = [keep.tile([P, PASSES, HALF], U32, name="wc_codes%d" % h, align_bytes=64) for h in range(2)]
         wc_scale = [keep.tile([P, PASSES, HALF], U8, name="wc_scale%d" % h, align_bytes=64) for h in range(2)]
         bias = keep.tile([P, NT], F32, name="bias")
+        edge_w = keep.tile([P, J], F32, name="edge_w")
         rows = [keep.tile([P, T], F32, name="rows%d" % i) for i in range(2)]
-        warm = stage.tile([P, 8], F32, name="late_f", align_bytes=64)
-        warm_out = stage.tile([P, 8], F32, name="late_w", align_bytes=64)
+        warm = keep.tile([P, 8], F32, name="warm")
+        warm_out = keep.tile([P, 8], F32, name="warm_out")
 
         nc.vector.memset(scale_win[:], 0)
         nc.vector.memset(warm[:], 0.0)
         nc.vector.memset(w_scale[:], 0)
         for c in range(CHUNKS):
             nc.vector.memset(s_scale[c][:], 0)
+        for i in range(2):
+            nc.vector.memset(rows[i][:], 0.0)
         nc.scalar.activation(warm_out[:], warm[:], ACT.Silu)
-        late_f = stage.tile([P, 2, J], F32, name="late_f", align_bytes=64)
-        late_w = stage.tile([P, 3, PASSES, N // 2], I32, name="late_w", align_bytes=64)
-        slot = [late_f[:, s, :] for s in range(2)]
-        w_words = [late_w[:, i, :, :] for i in range(3)]
-        wc_slot = {(0, 0): 0, (0, 1): 1, (1, 0): 0, (1, 1): 0}
-        edge_w = slot[1]
-
-        nc.sync.dma_start(lists[TGT][:], offs2)
-        nc.sync.dma_start(lists[SRC][:], offs)
-        for q in range(4):
-            nc.sync.dma_start(scale_win[32 * q : 32 * q + 8, :], tab_scales[:, 4 * q : 4 * q + 4, :].bitcast(I32))
-        nc.sync.dma_start(words[:], tab_words[0].rearrange("p t b -> p (t b)").bitcast(I32))
 
         def load_scales(i, scales, queue):
             for q in range(4):
@@ -78,26 +70,13 @@ def tile_list_rgg_ownsilu_kernel(
                 )
 
         def load_words(i, w):
-            nc.sync.dma_start(w_words[i], w.rearrange("a p n -> p a n").bitcast(I32))
+            nc.sync.dma_start(w_words[i][:], w.rearrange("a p n -> p a n").bitcast(I32))
 
         def load_wc(h, a):
             nc.sync.dma_start(
-                slot[wc_slot[h, a]].rearrange("p (i n) -> p i n", i=4),
+                wc_raw[h][:, a, :].rearrange("p (i n) -> p i n", i=4),
                 wc[512 * a : 512 * (a + 1), HALF * h : HALF * (h + 1)].rearrange("(p i) n -> p i n", i=4),
             )
-
-        load_wc(0, 0)
-        load_words(0, wa_words)
-        load_words(1, wb_words)
-        load_wc(0, 1)
-        load_scales(0, wa_scales, nc.sync)
-        load_scales(1, wb_scales, nc.sync)
-        load_words(2, wo_words)
-        load_scales(2, wo_scales, nc.gpsimd)
-        with nc.allow_non_contiguous_dma("one bias value a partition"):
-            nc.gpsimd.dma_start(bias[:], b.rearrange("(t p) -> p t", p=P))
-        for i in range(2):
-            nc.gpsimd.memset(rows[i][:], 0.0)
 
         def piece(l, c):
             return lists[l][:, c * (CH // 16) : (c + 1) * (CH // 16)]
@@ -107,17 +86,18 @@ def tile_list_rgg_ownsilu_kernel(
                 nc.vector.tensor_copy(g_scale[c][:, l, :].bitcast(U8), scale_win[:].bitcast(U8).indirect(piece(l, c)))
             nc.sync.dma_start(s_scale[c][0:112, :, :], g_scale[c][4:116, :, :])
 
-        def gather_words(c):
-            for l in (TGT, SRC):
-                nc.vector.tensor_copy(g_words[c][l][:], words[:].bitcast(U32).indirect(piece(l, c)))
-            for l in (TGT, SRC):
-                nc.vector.tensor_copy(
-                    parted[c][l][:].bitcast(U16),
-                    g_words[c][l][:].bitcast(U16).rearrange("p (j d) -> p d j", d=2),
-                )
+        def gather_words(c, l):
+            nc.vector.tensor_copy(g_words[c, l][:], words[:].bitcast(U32).indirect(piece(l, c)))
 
-        def group_wc(h, a):
-            nc.scalar.copy(wc_grp[h][:, a, :, :], slot[wc_slot[h, a]].rearrange("p (i n) -> p n i", i=4))
+        def part_words(c, l):
+            nc.vector.tensor_copy(
+                parted[c][l][:].bitcast(U16),
+                g_words[c, l][:].bitcast(U16).rearrange("p (j d) -> p d j", d=2),
+            )
+
+        def group_wc(h):
+            for a in range(PASSES):
+                nc.scalar.copy(wc_grp[h][:, a, :, :], wc_raw[h][:, a, :].rearrange("p (i n) -> p n i", i=4))
 
         def quantize_wc(h):
             nc.vector.quantize_mx(
@@ -146,52 +126,85 @@ def tile_list_rgg_ownsilu_kernel(
                     out=acc[:], lhsT=w, lhsT_scale=ws, rhs=v, rhs_scale=vs, start=(i == 0), stop=(i == len(pairs) - 1)
                 )
 
-        def front(nt, c, first=False):
+        def message(nt, c, on_vector, th=None):
             za = psum.tile([P, CH], F32, name="za")
             ms = psum.tile([P, CH], F32, name="ms", bufs=3)
-            ow = psum.tile([P, CH], F32, name="ow", bufs=3)
             product(za, [(packed_weight(i, a, nt), table(c, l, a)) for a in range(PASSES) for i, l in ((0, TGT), (1, SRC))])
             product(ms, [(wc_weight(a, nt), table(c, SRC, a)) for a in range(PASSES)])
-            product(ow, [(packed_weight(2, a, nt), table(c, TGT, a)) for a in range(PASSES)])
-            th = ring.tile([P, CH], F32, name="th")
+            if th is None:
+                th = ring.tile([P, CH], F32, name="th")
             nc.scalar.activation(th[:], za[:], ACT.Tanh, scale=0.5)
             msg = ring.tile([P, CH], F32, name="msg")
-            nc.vector.scalar_tensor_tensor(msg[:], th[:], 1.0, ms[:], ALU.add, ALU.mult)
-            both = ring.tile([P, CH], F32, name="both")
-            if first:
-                nc.vector.scalar_tensor_tensor(both[:], ow[:], 2.0, msg[:], ALU.mult, ALU.add)
+            if on_vector:
+                nc.vector.scalar_tensor_tensor(msg[:], th[:], 1.0, ms[:], ALU.add, ALU.mult)
             else:
-                own = ring.tile([P, CH], F32, name="own")
-                nc.scalar.activation(own[:], ow[:], ACT.Copy, scale=2.0)
-                nc.gpsimd.tensor_tensor(both[:], msg[:], own[:], ALU.add)
+                gate = ring.tile([P, CH], F32, name="gate")
+                nc.scalar.activation(gate[:], th[:], ACT.Identity, bias=1.0)
+                raw = ring.tile([P, CH], F32, name="raw")
+                nc.scalar.copy(raw[:], ms[:])
+                nc.gpsimd.tensor_tensor(msg[:], gate[:], raw[:], ALU.mult)
+            return msg
+
+        def finish(nt, c, msg, last):
+            ow = psum.tile([P, CH], F32, name="ow", bufs=3)
+            product(ow, [(packed_weight(2, a, nt), table(c, TGT, a)) for a in range(PASSES)])
+            both = ring.tile([P, CH], F32, name="both")
+            own = ring.tile([P, CH], F32, name="own")
+            nc.scalar.activation(own[:], ow[:], ACT.Copy, scale=2.0)
+            nc.gpsimd.tensor_tensor(both[:], msg[:], own[:], ALU.add)
             act = ring.tile([P, CH], F32, name="act")
             nc.scalar.activation(act[:], both[:], ACT.Silu, bias=bias[:, nt : nt + 1], scale=0.5)
-            val = ring.tile([P, CH], F32, name="val", bufs=4)
-            (nc.vector if first else nc.gpsimd).tensor_tensor(val[:], act[:], edge_w[:, c * CH : (c + 1) * CH], ALU.mult)
-            return val
-
-        def back(nt, c, val):
-            nc.vector.tensor_copy(rows[nt % 2][:].indirect(piece(TGT, c)), val[:])
+            window = rows[nt % 2][:].indirect(piece(TGT, c))
+            weight = edge_w[:, c * CH : (c + 1) * CH]
+            if last:
+                nc.vector.tensor_tensor(window, act[:], weight, ALU.mult)
+            else:
+                val = ring.tile([P, CH], F32, name="val", bufs=4)
+                nc.gpsimd.tensor_tensor(val[:], act[:], weight, ALU.mult)
+                nc.vector.tensor_copy(window, val[:])
             if c == CHUNKS - 1:
                 nc.sync.dma_start(out[nt * P : (nt + 1) * P, :], rows[nt % 2][:])
 
+        nc.sync.dma_start(lists[TGT][:], offs2)
+        nc.sync.dma_start(lists[SRC][:], offs)
+        for q in range(4):
+            nc.sync.dma_start(scale_win[32 * q : 32 * q + 8, :], tab_scales[:, 4 * q : 4 * q + 4, :].bitcast(I32))
+        nc.sync.dma_start(words[:], tab_words[0].rearrange("p t b -> p (t b)").bitcast(I32))
+        load_scales(2, wo_scales, nc.gpsimd)
+        with nc.allow_non_contiguous_dma("one bias value a partition"):
+            nc.gpsimd.dma_start(bias[:], b.rearrange("(t p) -> p t", p=P))
+        load_wc(0, 0)
+        load_scales(0, wa_scales, nc.sync)
+        load_wc(0, 1)
+        load_words(0, wa_words)
+        load_words(1, wb_words)
+        load_scales(1, wb_scales, nc.sync)
         gather_scales(0)
-        gather_words(0)
-        group_wc(0, 0)
-        group_wc(0, 1)
-        gather_scales(1)
-        quantize_wc(0)
+        load_words(2, wo_words)
         load_wc(1, 0)
-        nc.sync.dma_start(edge_w, wgo)
-        group_wc(1, 0)
         load_wc(1, 1)
-        group_wc(1, 1)
-        units = [(nt, c) for nt in range(NT) for c in range(CHUNKS)]
-        vals = {0: front(*units[0], first=True)}
-        gather_words(1)
-        vals[1] = front(*units[1])
-        quantize_wc(1)
-        for u in range(len(units)):
-            if u + 2 < len(units):
-                vals[u + 2] = front(*units[u + 2])
-            back(*units[u], vals[u])
+        nc.sync.dma_start(edge_w[:], wgo)
+        gather_words(0, TGT)
+        gather_words(0, SRC)
+        part_words(0, TGT)
+        part_words(0, SRC)
+        group_wc(0)
+        quantize_wc(0)
+        g_scale[1] = keep.tile([P, 2, CH // 4], I32, name="wc_grp0", align_bytes=64)
+        gather_scales(1)
+        g_words[1, TGT] = keep.tile([P, CH], U32, name="wc_raw0", align_bytes=64)
+        gather_words(1, TGT)
+        part_words(1, TGT)
+        units = [(0, 0), (1, 0), (0, 1), (1, 1), (2, 0), (2, 1), (3, 0), (3, 1)]
+        on_vector = (0, 1, 4)
+        for u, (nt, c) in enumerate(units):
+            first_th = keep.tile([P, CH], F32, name="first_th", align_bytes=64) if u == 0 else None
+            msg = message(nt, c, u in on_vector, first_th)
+            if u == 0:
+                g_words[1, SRC] = keep.tile([P, CH], U32, name="first_th", align_bytes=64)
+                gather_words(1, SRC)
+                part_words(1, SRC)
+            finish(nt, c, msg, u == len(units) - 1)
+            if u == 1:
+                group_wc(1)
+                quantize_wc(1)

@@ -41,7 +41,7 @@ def tile_list_rgg_ownsilu_kernel(
         w_words = [keep.tile([P, PASSES, N // 2], I32, name="w_words%d" % i, align_bytes=64) for i in range(3)]
         g_scale = {0: keep.tile([P, 2, CH // 4], I32, name="g_scale0", align_bytes=64)}
         s_scale = [keep.tile([P, 2, CH // 4], I32, name="s_scale%d" % c, align_bytes=64) for c in range(CHUNKS)]
-        g_words = {(0, l): keep.tile([P, CH], U32, name="g_words0%d" % l, align_bytes=64) for l in range(2)}
+        g_words = {0: keep.tile([P, 2, CH], U32, name="g_words0", align_bytes=64)}
         parted = [[keep.tile([P, PASSES, 2 * CH], U8, name="parted%d%d" % (c, l), align_bytes=64) for l in range(2)] for c in range(CHUNKS)]
         wc_raw = [keep.tile([P, PASSES, 4 * HALF], F32, name="wc_raw%d" % h, align_bytes=64) for h in range(2)]
         wc_grp = [keep.tile([P, PASSES, HALF, 4], BF16, name="wc_grp%d" % h, align_bytes=64) for h in range(2)]
@@ -87,12 +87,12 @@ def tile_list_rgg_ownsilu_kernel(
             nc.sync.dma_start(s_scale[c][0:112, :, :], g_scale[c][4:116, :, :])
 
         def gather_words(c, l):
-            nc.vector.tensor_copy(g_words[c, l][:], words[:].bitcast(U32).indirect(piece(l, c)))
+            nc.vector.tensor_copy(g_words[c][:, l, :], words[:].bitcast(U32).indirect(piece(l, c)))
 
         def part_words(c, l):
             nc.vector.tensor_copy(
                 parted[c][l][:].bitcast(U16),
-                g_words[c, l][:].bitcast(U16).rearrange("p (j d) -> p d j", d=2),
+                g_words[c][:, l, :].bitcast(U16).rearrange("p (j d) -> p d j", d=2),
             )
 
         def group_wc(h):
@@ -126,41 +126,32 @@ def tile_list_rgg_ownsilu_kernel(
                     out=acc[:], lhsT=w, lhsT_scale=ws, rhs=v, rhs_scale=vs, start=(i == 0), stop=(i == len(pairs) - 1)
                 )
 
-        def message(nt, c, on_vector, th=None):
+        def front(nt, c, fused):
             za = psum.tile([P, CH], F32, name="za")
-            ms = psum.tile([P, CH], F32, name="ms", bufs=3)
+            ms = psum.tile([P, CH], F32, name="ms")
+            ow = psum.tile([P, CH], F32, name="ow")
             product(za, [(packed_weight(i, a, nt), table(c, l, a)) for a in range(PASSES) for i, l in ((0, TGT), (1, SRC))])
             product(ms, [(wc_weight(a, nt), table(c, SRC, a)) for a in range(PASSES)])
-            if th is None:
-                th = ring.tile([P, CH], F32, name="th")
+            product(ow, [(packed_weight(2, a, nt), table(c, TGT, a)) for a in range(PASSES)])
+            th = ring.tile([P, CH], F32, name="th")
             nc.scalar.activation(th[:], za[:], ACT.Tanh, scale=0.5)
             msg = ring.tile([P, CH], F32, name="msg")
-            if on_vector:
-                nc.vector.scalar_tensor_tensor(msg[:], th[:], 1.0, ms[:], ALU.add, ALU.mult)
-            else:
-                gate = ring.tile([P, CH], F32, name="gate")
-                nc.scalar.activation(gate[:], th[:], ACT.Identity, bias=1.0)
-                raw = ring.tile([P, CH], F32, name="raw")
-                nc.scalar.copy(raw[:], ms[:])
-                nc.gpsimd.tensor_tensor(msg[:], gate[:], raw[:], ALU.mult)
-            return msg
-
-        def finish(nt, c, msg, last):
-            ow = psum.tile([P, CH], F32, name="ow", bufs=3)
-            product(ow, [(packed_weight(2, a, nt), table(c, TGT, a)) for a in range(PASSES)])
+            nc.vector.scalar_tensor_tensor(msg[:], th[:], 1.0, ms[:], ALU.add, ALU.mult)
             both = ring.tile([P, CH], F32, name="both")
-            own = ring.tile([P, CH], F32, name="own")
-            nc.scalar.activation(own[:], ow[:], ACT.Copy, scale=2.0)
-            nc.gpsimd.tensor_tensor(both[:], msg[:], own[:], ALU.add)
-            act = ring.tile([P, CH], F32, name="act")
+            nc.vector.scalar_tensor_tensor(both[:], ow[:], 2.0, msg[:], ALU.mult, ALU.add)
+            act = ring.tile([P, CH], F32, name="act", bufs=4)
             nc.scalar.activation(act[:], both[:], ACT.Silu, bias=bias[:, nt : nt + 1], scale=0.5)
+            if fused:
+                return act
+            val = ring.tile([P, CH], F32, name="val")
+            nc.vector.tensor_tensor(val[:], act[:], edge_w[:, c * CH : (c + 1) * CH], ALU.mult)
+            return val
+
+        def back(nt, c, val, fused):
             window = rows[nt % 2][:].indirect(piece(TGT, c))
-            weight = edge_w[:, c * CH : (c + 1) * CH]
-            if last:
-                nc.vector.tensor_tensor(window, act[:], weight, ALU.mult)
+            if fused:
+                nc.vector.tensor_tensor(window, val[:], edge_w[:, c * CH : (c + 1) * CH], ALU.mult)
             else:
-                val = ring.tile([P, CH], F32, name="val", bufs=4)
-                nc.gpsimd.tensor_tensor(val[:], act[:], weight, ALU.mult)
                 nc.vector.tensor_copy(window, val[:])
             if c == CHUNKS - 1:
                 nc.sync.dma_start(out[nt * P : (nt + 1) * P, :], rows[nt % 2][:])
@@ -192,19 +183,16 @@ def tile_list_rgg_ownsilu_kernel(
         quantize_wc(0)
         g_scale[1] = keep.tile([P, 2, CH // 4], I32, name="wc_grp0", align_bytes=64)
         gather_scales(1)
-        g_words[1, TGT] = keep.tile([P, CH], U32, name="wc_raw0", align_bytes=64)
+        g_words[1] = keep.tile([P, 2, CH], U32, name="wc_raw0", align_bytes=64)
         gather_words(1, TGT)
+        gather_words(1, SRC)
         part_words(1, TGT)
+        part_words(1, SRC)
         units = [(0, 0), (1, 0), (0, 1), (1, 1), (2, 0), (2, 1), (3, 0), (3, 1)]
-        on_vector = (0, 1, 4)
-        for u, (nt, c) in enumerate(units):
-            first_th = keep.tile([P, CH], F32, name="first_th", align_bytes=64) if u == 0 else None
-            msg = message(nt, c, u in on_vector, first_th)
-            if u == 0:
-                g_words[1, SRC] = keep.tile([P, CH], U32, name="first_th", align_bytes=64)
-                gather_words(1, SRC)
-                part_words(1, SRC)
-            finish(nt, c, msg, u == len(units) - 1)
-            if u == 1:
-                group_wc(1)
-                quantize_wc(1)
+        vals = {0: front(*units[0], True), 1: front(*units[1], False)}
+        group_wc(1)
+        quantize_wc(1)
+        for u in range(len(units)):
+            if u + 2 < len(units):
+                vals[u + 2] = front(*units[u + 2], u % 2 == 0)
+            back(*units[u], vals[u], u % 2 == 0)

@@ -17,12 +17,25 @@ ALU = mybir.AluOpType
 ACT = mybir.ActivationFunctionType
 
 P = 128
-PASSES = 2
-CH = 512
-CHUNKS = J // CH
-NT = N // P
-HALF = 256
+PACK = 4
+PASSES = K // (P * PACK)
+QUADS = 4
+EDGES = 512
+TILES = N // P
+HALF = N // 2
 SRC, TGT = 0, 1
+WA, WB, WO = 0, 1, 2
+ALIGN = 64
+MOVED = 112
+WINDOWS = 3
+RING = 3
+
+UNITS = ((1, 0), (0, 0), (0, 1), (2, 1), (1, 1), (3, 0), (2, 0), (3, 1))
+BATCHES = ((0, 1), (2,), (3, 4, 5), (6, 7))
+GATE_ON_VECTOR = (0, 1, 4, 5)
+SUM_ON_VECTOR = (0, 1, 3)
+WEIGHT_ON_VECTOR = (0,)
+WEIGHT_IN_SCATTER = (6, 7)
 
 
 def tile_list_rgg_ownsilu_kernel(
@@ -31,168 +44,211 @@ def tile_list_rgg_ownsilu_kernel(
     nc = tc.nc
     with ExitStack() as ctx:
         keep = ctx.enter_context(tc.tile_pool(name="keep", bufs=1))
-        ring = ctx.enter_context(tc.tile_pool(name="ring", bufs=3))
-        psum = ctx.enter_context(tc.psum_pool(name="psum", bufs=2))
+        ring = ctx.enter_context(tc.tile_pool(name="ring", bufs=RING))
+        psum = ctx.enter_context(tc.psum_pool(name="psum", bufs=3))
 
-        lists = [keep.tile([P, J // 16], U16, name="list_src"), keep.tile([P, J // 16], U16, name="list_tgt")]
-        words = keep.tile([P, T], I32, name="words", align_bytes=64)
-        scale_win = keep.tile([P, T // 4], I32, name="scale_win", align_bytes=64)
-        w_scale = keep.tile([P, 3, PASSES, N // 4], I32, name="w_scale", align_bytes=64)
-        w_words = [keep.tile([P, PASSES, N // 2], I32, name="w_words%d" % i, align_bytes=64) for i in range(3)]
-        g_scale = {0: keep.tile([P, 2, CH // 4], I32, name="g_scale0", align_bytes=64)}
-        s_scale = [keep.tile([P, 2, CH // 4], I32, name="s_scale%d" % c, align_bytes=64) for c in range(CHUNKS)]
-        g_words = {0: keep.tile([P, 2, CH], U32, name="g_words0", align_bytes=64)}
-        parted = [[keep.tile([P, PASSES, 2 * CH], U8, name="parted%d%d" % (c, l), align_bytes=64) for l in range(2)] for c in range(CHUNKS)]
-        wc_raw = [keep.tile([P, PASSES, 4 * HALF], F32, name="wc_raw%d" % h, align_bytes=64) for h in range(2)]
-        wc_grp = [keep.tile([P, PASSES, HALF, 4], BF16, name="wc_grp%d" % h, align_bytes=64) for h in range(2)]
-        wc_codes = [keep.tile([P, PASSES, HALF], U32, name="wc_codes%d" % h, align_bytes=64) for h in range(2)]
-        wc_scale = [keep.tile([P, PASSES, HALF], U8, name="wc_scale%d" % h, align_bytes=64) for h in range(2)]
-        bias = keep.tile([P, NT], F32, name="bias")
+        lists = [keep.tile([P, J // 16], U16, name="list%d" % side) for side in (SRC, TGT)]
+        words = keep.tile([P, T], I32, name="words", align_bytes=ALIGN)
+        scales = keep.tile([P, T // 4], I32, name="scales", align_bytes=ALIGN)
+        w_words = [keep.tile([P, PASSES, N // 2], I32, name="w_words%d" % w, align_bytes=ALIGN) for w in (WA, WB, WO)]
+        w_scales = keep.tile([P, 3, PASSES, N // 4], I32, name="w_scales", align_bytes=ALIGN)
+        picked_scales = [keep.tile([P, 2, J // 4], I32, name="picked_scales%d" % a, align_bytes=ALIGN) for a in range(PASSES)]
+        picked_words = {
+            (half, side): keep.tile([P, PASSES, 2 * EDGES], U8, name="picked_words%d%d" % (half, side), align_bytes=ALIGN)
+            for half in range(2)
+            for side in (SRC, TGT)
+        }
+        wc_raw = [keep.tile([P, PASSES, PACK * HALF], F32, name="wc_raw%d" % h, align_bytes=ALIGN) for h in range(2)]
+        wc_bf16 = [keep.tile([P, PASSES, P, PACK], BF16, name="wc_bf16%d" % t, align_bytes=ALIGN) for t in range(TILES)]
+        wc_codes = [keep.tile([P, PASSES, P], U32, name="wc_codes%d" % t, align_bytes=ALIGN) for t in range(TILES)]
+        wc_scales = [keep.tile([P, PASSES, P], U8, name="wc_scales%d" % t, align_bytes=ALIGN) for t in range(TILES)]
+        bias = keep.tile([P, TILES], F32, name="bias")
         edge_w = keep.tile([P, J], F32, name="edge_w")
-        rows = [keep.tile([P, T], F32, name="rows%d" % i) for i in range(2)]
-        warm = keep.tile([P, 8], F32, name="warm")
-        warm_out = keep.tile([P, 8], F32, name="warm_out")
+        windows = [keep.tile([P, T], F32, name="window%d" % i) for i in range(WINDOWS)]
+        silu_in = keep.tile([P, 1], F32, name="silu_in")
+        zero = keep.tile([P, 1], F32, name="zero")
 
-        nc.vector.memset(scale_win[:], 0)
-        nc.vector.memset(warm[:], 0.0)
-        nc.vector.memset(w_scale[:], 0)
-        for c in range(CHUNKS):
-            nc.vector.memset(s_scale[c][:], 0)
-        for i in range(2):
-            nc.vector.memset(rows[i][:], 0.0)
-        nc.scalar.activation(warm_out[:], warm[:], ACT.Silu)
+        nc.gpsimd.memset(scales[:], 0)
+        nc.gpsimd.memset(silu_in[:], 0.0)
+        nc.gpsimd.memset(w_scales[:], 0)
+        nc.gpsimd.memset(picked_scales[1][:], 0)
+        for window in windows:
+            nc.gpsimd.memset(window[:], 0.0)
+        nc.scalar.activation(zero[:], silu_in[:], ACT.Silu)
 
-        def load_scales(i, scales, queue):
-            for q in range(4):
-                queue.dma_start(
-                    w_scale[32 * q : 32 * q + 4, i, :, :],
-                    scales[:, 4 * q : 4 * q + 4, :].rearrange("a r n -> r a n").bitcast(I32),
+        def load_packed(w, w_dram):
+            nc.sync.dma_start(w_words[w][:], w_dram.rearrange("a p n -> p a n").bitcast(I32))
+
+        def load_scale_rows(w, s_dram):
+            for q in range(QUADS):
+                nc.sync.dma_start(
+                    w_scales[32 * q : 32 * q + 4, w, :, :],
+                    s_dram[:, 4 * q : 4 * q + 4, :].rearrange("a r n -> r a n").bitcast(I32),
                 )
-
-        def load_words(i, w):
-            nc.sync.dma_start(w_words[i][:], w.rearrange("a p n -> p a n").bitcast(I32))
 
         def load_wc(h, a):
-            nc.sync.dma_start(
-                wc_raw[h][:, a, :].rearrange("p (i n) -> p i n", i=4),
-                wc[512 * a : 512 * (a + 1), HALF * h : HALF * (h + 1)].rearrange("(p i) n -> p i n", i=4),
-            )
+            rows = wc[P * PACK * a : P * PACK * (a + 1), HALF * h : HALF * (h + 1)]
+            nc.sync.dma_start(wc_raw[h][:, a, :].rearrange("p (i n) -> p i n", i=PACK), rows.rearrange("(p i) n -> p i n", i=PACK))
 
-        def piece(l, c):
-            return lists[l][:, c * (CH // 16) : (c + 1) * (CH // 16)]
+        def list_half(side, half):
+            return lists[side][:, half * (EDGES // 16) : (half + 1) * (EDGES // 16)]
 
-        def gather_scales(c):
-            for l in (TGT, SRC):
-                nc.vector.tensor_copy(g_scale[c][:, l, :].bitcast(U8), scale_win[:].bitcast(U8).indirect(piece(l, c)))
-            nc.sync.dma_start(s_scale[c][0:112, :, :], g_scale[c][4:116, :, :])
+        def gather_scales():
+            for side in (TGT, SRC):
+                nc.vector.tensor_copy(picked_scales[0][:, side, :].bitcast(U8), scales[:].bitcast(U8).indirect(lists[side][:]))
+            nc.sync.dma_start(picked_scales[1][0:MOVED, :, :], picked_scales[0][4 : 4 + MOVED, :, :])
 
-        def gather_words(c, l):
-            nc.vector.tensor_copy(g_words[c][:, l, :], words[:].bitcast(U32).indirect(piece(l, c)))
+        def gather_words(half, side, slot):
+            pairs = keep.tile([P, EDGES], U32, name=slot, align_bytes=ALIGN)
+            nc.vector.tensor_copy(pairs[:], words[:].bitcast(U32).indirect(list_half(side, half)))
+            return pairs
 
-        def part_words(c, l):
+        def part_words(half, side, pairs):
             nc.vector.tensor_copy(
-                parted[c][l][:].bitcast(U16),
-                g_words[c][:, l, :].bitcast(U16).rearrange("p (j d) -> p d j", d=2),
+                picked_words[half, side][:].bitcast(U16), pairs[:].bitcast(U16).rearrange("p (j a) -> p a j", a=PASSES)
             )
 
-        def group_wc(h):
+        def interleave_wc(t):
+            h, first = divmod(t * P, HALF)
             for a in range(PASSES):
-                nc.scalar.copy(wc_grp[h][:, a, :, :], wc_raw[h][:, a, :].rearrange("p (i n) -> p n i", i=4))
+                nc.scalar.copy(wc_bf16[t][:, a, :, :], wc_raw[h][:, a, :].rearrange("p (i n) -> p n i", i=PACK)[:, first : first + P, :])
 
-        def quantize_wc(h):
+        def quantize_wc(t):
             nc.vector.quantize_mx(
-                out=wc_codes[h][:].rearrange("p a n -> p (a n)").bitcast(FP8X4),
-                scales=wc_scale[h][:].rearrange("p a n -> p (a n)"),
-                in_=wc_grp[h][:].rearrange("p a n i -> p (a n i)"),
+                out=wc_codes[t][:].rearrange("p a n -> p (a n)").bitcast(FP8X4),
+                scales=wc_scales[t][:].rearrange("p a n -> p (a n)"),
+                in_=wc_bf16[t][:].rearrange("p a n i -> p (a n i)"),
             )
 
-        def table(c, l, a):
-            plane = g_scale[c] if a == 0 else s_scale[c]
-            return parted[c][l][:, a, :].bitcast(FP4X4), plane[:, l, :].bitcast(U8)
+        def table_operand(half, side, a):
+            plane = picked_scales[a][:, side, half * EDGES // 4 : (half + 1) * EDGES // 4]
+            return picked_words[half, side][:, a, :].bitcast(FP4X4), plane.bitcast(U8)
 
-        def packed_weight(i, a, nt):
-            return (
-                w_words[i][:, a, 64 * nt : 64 * (nt + 1)].bitcast(FP4X4),
-                w_scale[:, i, a, 32 * nt : 32 * (nt + 1)].bitcast(U8),
-            )
+        def packed_operand(w, a, t):
+            codes = w_words[w][:, a, t * P // 2 : (t + 1) * P // 2]
+            plane = w_scales[:, w, a, t * P // 4 : (t + 1) * P // 4]
+            return codes.bitcast(FP4X4), plane.bitcast(U8)
 
-        def wc_weight(a, nt):
-            h, o = divmod(nt * P, HALF)
-            return wc_codes[h][:, a, o : o + P].bitcast(FP8X4), wc_scale[h][:, a, o : o + P]
+        def wc_operand(a, t):
+            return wc_codes[t][:, a, :].bitcast(FP8X4), wc_scales[t][:, a, :]
 
-        def product(acc, pairs):
-            for i, ((w, ws), (v, vs)) in enumerate(pairs):
+        def accumulate(acc, operand_pairs):
+            for i, ((lhs, lhs_scale), (rhs, rhs_scale)) in enumerate(operand_pairs):
                 nc.tensor.matmul_mx(
-                    out=acc[:], lhsT=w, lhsT_scale=ws, rhs=v, rhs_scale=vs, start=(i == 0), stop=(i == len(pairs) - 1)
+                    out=acc[:],
+                    lhsT=lhs,
+                    lhsT_scale=lhs_scale,
+                    rhs=rhs,
+                    rhs_scale=rhs_scale,
+                    start=(i == 0),
+                    stop=(i == len(operand_pairs) - 1),
                 )
 
-        def front(nt, c, fused):
-            za = psum.tile([P, CH], F32, name="za")
-            ms = psum.tile([P, CH], F32, name="ms")
-            ow = psum.tile([P, CH], F32, name="ow")
-            product(za, [(packed_weight(i, a, nt), table(c, l, a)) for a in range(PASSES) for i, l in ((0, TGT), (1, SRC))])
-            product(ms, [(wc_weight(a, nt), table(c, SRC, a)) for a in range(PASSES)])
-            product(ow, [(packed_weight(2, a, nt), table(c, TGT, a)) for a in range(PASSES)])
-            th = ring.tile([P, CH], F32, name="th")
-            nc.scalar.activation(th[:], za[:], ACT.Tanh, scale=0.5)
-            msg = ring.tile([P, CH], F32, name="msg")
-            nc.vector.scalar_tensor_tensor(msg[:], th[:], 1.0, ms[:], ALU.add, ALU.mult)
-            both = ring.tile([P, CH], F32, name="both")
-            nc.vector.scalar_tensor_tensor(both[:], ow[:], 2.0, msg[:], ALU.mult, ALU.add)
-            act = ring.tile([P, CH], F32, name="act", bufs=4)
-            nc.scalar.activation(act[:], both[:], ACT.Silu, bias=bias[:, nt : nt + 1], scale=0.5)
-            if fused:
-                return act
-            val = ring.tile([P, CH], F32, name="val")
-            nc.vector.tensor_tensor(val[:], act[:], edge_w[:, c * CH : (c + 1) * CH], ALU.mult)
-            return val
+        messages, values = {}, {}
 
-        def back(nt, c, val, fused):
-            window = rows[nt % 2][:].indirect(piece(TGT, c))
-            if fused:
-                nc.vector.tensor_tensor(window, val[:], edge_w[:, c * CH : (c + 1) * CH], ALU.mult)
+        def message(u):
+            t, half = UNITS[u]
+            za = psum.tile([P, EDGES], F32, name="za")
+            ms = psum.tile([P, EDGES], F32, name="ms")
+            accumulate(
+                za,
+                [
+                    (packed_operand(w, a, t), table_operand(half, side, a))
+                    for w, side in ((WA, TGT), (WB, SRC))
+                    for a in range(PASSES)
+                ],
+            )
+            accumulate(ms, [(wc_operand(a, t), table_operand(half, SRC, a)) for a in range(PASSES)])
+            tanh = ring.tile([P, EDGES], F32, name="tanh")
+            nc.scalar.activation(tanh[:], za[:], ACT.Tanh, bias=zero[:], scale=0.5)
+            gated = ring.tile([P, EDGES], F32, name="gated")
+            if u in GATE_ON_VECTOR:
+                nc.vector.scalar_tensor_tensor(gated[:], tanh[:], 1.0, ms[:], ALU.add, ALU.mult)
             else:
-                nc.vector.tensor_copy(window, val[:])
-            if c == CHUNKS - 1:
-                nc.sync.dma_start(out[nt * P : (nt + 1) * P, :], rows[nt % 2][:])
+                gate = ring.tile([P, EDGES], F32, name="gate")
+                nc.scalar.activation(gate[:], tanh[:], ACT.Identity, bias=1.0)
+                ms_copy = ring.tile([P, EDGES], F32, name="ms_copy")
+                nc.scalar.copy(ms_copy[:], ms[:])
+                nc.gpsimd.tensor_tensor(gated[:], gate[:], ms_copy[:], ALU.mult)
+            messages[u] = gated
+
+        def weight_of(u):
+            half = UNITS[u][1]
+            return edge_w[:, half * EDGES : (half + 1) * EDGES]
+
+        def value(u):
+            t, half = UNITS[u]
+            ow = psum.tile([P, EDGES], F32, name="ow", bufs=2)
+            accumulate(ow, [(packed_operand(WO, a, t), table_operand(half, TGT, a)) for a in range(PASSES)])
+            twice = ring.tile([P, EDGES], F32, name="twice")
+            if u in SUM_ON_VECTOR:
+                nc.vector.scalar_tensor_tensor(twice[:], ow[:], 2.0, messages[u][:], ALU.mult, ALU.add)
+            else:
+                ow_twice = ring.tile([P, EDGES], F32, name="ow_twice")
+                nc.scalar.activation(ow_twice[:], ow[:], ACT.Copy, scale=2.0)
+                nc.gpsimd.tensor_tensor(twice[:], messages[u][:], ow_twice[:], ALU.add)
+            silu = ring.tile([P, EDGES], F32, name="silu")
+            nc.scalar.activation(silu[:], twice[:], ACT.Silu, bias=bias[:, t : t + 1], scale=0.5)
+            if u in WEIGHT_IN_SCATTER:
+                values[u] = silu
+            else:
+                weighted = ring.tile([P, EDGES], F32, name="weighted", bufs=len(UNITS) - len(WEIGHT_IN_SCATTER))
+                engine = nc.vector if u in WEIGHT_ON_VECTOR else nc.gpsimd
+                engine.tensor_tensor(weighted[:], silu[:], weight_of(u), ALU.mult)
+                values[u] = weighted
+
+        def scatter(u):
+            t, half = UNITS[u]
+            window = windows[t % WINDOWS]
+            places = window[:].indirect(list_half(TGT, half))
+            if u in WEIGHT_IN_SCATTER:
+                nc.vector.tensor_tensor(places, values[u][:], weight_of(u), ALU.mult)
+            else:
+                nc.vector.tensor_copy(places, values[u][:])
+            if all(later[0] != t for later in UNITS[u + 1 :]):
+                nc.sync.dma_start(out[t * P : (t + 1) * P, :], window[:])
 
         nc.sync.dma_start(lists[TGT][:], offs2)
         nc.sync.dma_start(lists[SRC][:], offs)
-        for q in range(4):
-            nc.sync.dma_start(scale_win[32 * q : 32 * q + 8, :], tab_scales[:, 4 * q : 4 * q + 4, :].bitcast(I32))
+        for q in range(QUADS):
+            nc.sync.dma_start(scales[32 * q : 32 * q + 8, :], tab_scales[:, 4 * q : 4 * q + 4, :].bitcast(I32))
         nc.sync.dma_start(words[:], tab_words[0].rearrange("p t b -> p (t b)").bitcast(I32))
-        load_scales(2, wo_scales, nc.gpsimd)
-        with nc.allow_non_contiguous_dma("one bias value a partition"):
-            nc.gpsimd.dma_start(bias[:], b.rearrange("(t p) -> p t", p=P))
-        load_wc(0, 0)
-        load_scales(0, wa_scales, nc.sync)
+        load_scale_rows(WA, wa_scales)
+        load_packed(WA, wa_words)
         load_wc(0, 1)
-        load_words(0, wa_words)
-        load_words(1, wb_words)
-        load_scales(1, wb_scales, nc.sync)
-        gather_scales(0)
-        load_words(2, wo_words)
-        load_wc(1, 0)
-        load_wc(1, 1)
+        load_packed(WO, wo_words)
         nc.sync.dma_start(edge_w[:], wgo)
-        gather_words(0, TGT)
-        gather_words(0, SRC)
-        part_words(0, TGT)
-        part_words(0, SRC)
-        group_wc(0)
-        quantize_wc(0)
-        g_scale[1] = keep.tile([P, 2, CH // 4], I32, name="wc_grp0", align_bytes=64)
-        gather_scales(1)
-        g_words[1] = keep.tile([P, 2, CH], U32, name="wc_raw0", align_bytes=64)
-        gather_words(1, TGT)
-        gather_words(1, SRC)
-        part_words(1, TGT)
-        part_words(1, SRC)
-        units = [(0, 0), (1, 0), (0, 1), (1, 1), (2, 0), (2, 1), (3, 0), (3, 1)]
-        vals = {0: front(*units[0], True), 1: front(*units[1], False)}
-        group_wc(1)
-        quantize_wc(1)
-        for u in range(len(units)):
-            if u + 2 < len(units):
-                vals[u + 2] = front(*units[u + 2], u % 2 == 0)
-            back(*units[u], vals[u], u % 2 == 0)
+        load_wc(1, 0)
+        gather_scales()
+        load_scale_rows(WB, wb_scales)
+        load_wc(0, 0)
+        load_packed(WB, wb_words)
+        load_scale_rows(WO, wo_scales)
+        load_wc(1, 1)
+        with nc.allow_non_contiguous_dma("one bias value for each partition and channel tile"):
+            nc.sync.dma_start(bias[:], b.rearrange("(t p) -> p t", p=P))
+
+        first_pairs = {side: gather_words(0, side, "pairs%d" % side) for side in (TGT, SRC)}
+        for side in (TGT, SRC):
+            part_words(0, side, first_pairs[side])
+        for t in range(TILES // 2):
+            interleave_wc(t)
+            quantize_wc(t)
+        part_words(1, SRC, gather_words(1, SRC, "pairs%d" % TGT))
+        part_words(1, TGT, gather_words(1, TGT, "wc_raw0"))
+        for u in BATCHES[0]:
+            message(u)
+        second_half = range(TILES - 1, TILES // 2 - 1, -1)
+        for t in second_half:
+            interleave_wc(t)
+        for u in BATCHES[0]:
+            value(u)
+        for t in second_half:
+            quantize_wc(t)
+        for batch in BATCHES[1:]:
+            for u in batch:
+                message(u)
+            for u in batch:
+                value(u)
+        for u in range(len(UNITS)):
+            scatter(u)

from contextlib import ExitStack

import concourse.mybir as mybir

K, N, T, J = 1024, 512, 2048, 1024
FLOPS = 4 * 2 * K * N * J

F32 = mybir.dt.float32
BF16 = mybir.dt.bfloat16
I32 = mybir.dt.int32
U32 = mybir.dt.uint32
U16 = mybir.dt.uint16
U8 = mybir.dt.uint8
FP8X4 = mybir.dt.float8_e4m3fn_x4
FP4X4 = mybir.dt.float4_e2m1fn_x4
ALU = mybir.AluOpType
ACT = mybir.ActivationFunctionType

P = 128
PACK = 4
PASSES = K // (P * PACK)
QUADS = 4
EDGES = 512
TILES = N // P
HALF = N // 2
SRC, TGT = 0, 1
WA, WB, WO = 0, 1, 2
ALIGN = 64
MOVED = 112
WINDOWS = 3
RING = 3

UNITS = ((1, 0), (0, 0), (0, 1), (2, 1), (1, 1), (3, 0), (2, 0), (3, 1))
BATCHES = ((0, 1), (2,), (3, 4, 5), (6, 7))
GATE_ON_VECTOR = (0, 1, 4, 5)
SUM_ON_VECTOR = (0, 1, 3)
WEIGHT_ON_VECTOR = (0,)
WEIGHT_IN_SCATTER = (6, 7)


def tile_list_rgg_ownsilu_kernel(
    tc, tab_words, tab_scales, wa_words, wa_scales, wb_words, wb_scales, wc, wo_words, wo_scales, b, wgo, offs, offs2, out
):
    nc = tc.nc
    with ExitStack() as ctx:
        keep = ctx.enter_context(tc.tile_pool(name="keep", bufs=1))
        ring = ctx.enter_context(tc.tile_pool(name="ring", bufs=RING))
        psum = ctx.enter_context(tc.psum_pool(name="psum", bufs=3))

        lists = [keep.tile([P, J // 16], U16, name="list%d" % side) for side in (SRC, TGT)]
        words = keep.tile([P, T], I32, name="words", align_bytes=ALIGN)
        scales = keep.tile([P, T // 4], I32, name="scales", align_bytes=ALIGN)
        w_words = [keep.tile([P, PASSES, N // 2], I32, name="w_words%d" % w, align_bytes=ALIGN) for w in (WA, WB, WO)]
        w_scales = keep.tile([P, 3, PASSES, N // 4], I32, name="w_scales", align_bytes=ALIGN)
        picked_scales = [keep.tile([P, 2, J // 4], I32, name="picked_scales%d" % a, align_bytes=ALIGN) for a in range(PASSES)]
        picked_words = {
            (half, side): keep.tile([P, PASSES, 2 * EDGES], U8, name="picked_words%d%d" % (half, side), align_bytes=ALIGN)
            for half in range(2)
            for side in (SRC, TGT)
        }
        wc_raw = [keep.tile([P, PASSES, PACK * HALF], F32, name="wc_raw%d" % h, align_bytes=ALIGN) for h in range(2)]
        wc_bf16 = [keep.tile([P, PASSES, P, PACK], BF16, name="wc_bf16%d" % t, align_bytes=ALIGN) for t in range(TILES)]
        wc_codes = [keep.tile([P, PASSES, P], U32, name="wc_codes%d" % t, align_bytes=ALIGN) for t in range(TILES)]
        wc_scales = [keep.tile([P, PASSES, P], U8, name="wc_scales%d" % t, align_bytes=ALIGN) for t in range(TILES)]
        bias = keep.tile([P, TILES], F32, name="bias")
        edge_w = keep.tile([P, J], F32, name="edge_w")
        windows = [keep.tile([P, T], F32, name="window%d" % i) for i in range(WINDOWS)]
        silu_in = keep.tile([P, 1], F32, name="silu_in")
        zero = keep.tile([P, 1], F32, name="zero")

        nc.gpsimd.memset(scales[:], 0)
        nc.gpsimd.memset(silu_in[:], 0.0)
        nc.gpsimd.memset(w_scales[:], 0)
        nc.gpsimd.memset(picked_scales[1][:], 0)
        for window in windows:
            nc.gpsimd.memset(window[:], 0.0)
        nc.scalar.activation(zero[:], silu_in[:], ACT.Silu)

        def load_packed(w, w_dram):
            nc.sync.dma_start(w_words[w][:], w_dram.rearrange("a p n -> p a n").bitcast(I32))

        def load_scale_rows(w, s_dram):
            for q in range(QUADS):
                nc.sync.dma_start(
                    w_scales[32 * q : 32 * q + 4, w, :, :],
                    s_dram[:, 4 * q : 4 * q + 4, :].rearrange("a r n -> r a n").bitcast(I32),
                )

        def load_wc(h, a):
            rows = wc[P * PACK * a : P * PACK * (a + 1), HALF * h : HALF * (h + 1)]
            nc.sync.dma_start(wc_raw[h][:, a, :].rearrange("p (i n) -> p i n", i=PACK), rows.rearrange("(p i) n -> p i n", i=PACK))

        def list_half(side, half):
            return lists[side][:, half * (EDGES // 16) : (half + 1) * (EDGES // 16)]

        def gather_scales():
            for side in (TGT, SRC):
                nc.vector.tensor_copy(picked_scales[0][:, side, :].bitcast(U8), scales[:].bitcast(U8).indirect(lists[side][:]))
            nc.sync.dma_start(picked_scales[1][0:MOVED, :, :], picked_scales[0][4 : 4 + MOVED, :, :])

        def gather_words(half, side, slot):
            pairs = keep.tile([P, EDGES], U32, name=slot, align_bytes=ALIGN)
            nc.vector.tensor_copy(pairs[:], words[:].bitcast(U32).indirect(list_half(side, half)))
            return pairs

        def part_words(half, side, pairs):
            nc.vector.tensor_copy(
                picked_words[half, side][:].bitcast(U16), pairs[:].bitcast(U16).rearrange("p (j a) -> p a j", a=PASSES)
            )

        def interleave_wc(t):
            h, first = divmod(t * P, HALF)
            for a in range(PASSES):
                nc.scalar.copy(wc_bf16[t][:, a, :, :], wc_raw[h][:, a, :].rearrange("p (i n) -> p n i", i=PACK)[:, first : first + P, :])

        def quantize_wc(t):
            nc.vector.quantize_mx(
                out=wc_codes[t][:].rearrange("p a n -> p (a n)").bitcast(FP8X4),
                scales=wc_scales[t][:].rearrange("p a n -> p (a n)"),
                in_=wc_bf16[t][:].rearrange("p a n i -> p (a n i)"),
            )

        def table_operand(half, side, a):
            plane = picked_scales[a][:, side, half * EDGES // 4 : (half + 1) * EDGES // 4]
            return picked_words[half, side][:, a, :].bitcast(FP4X4), plane.bitcast(U8)

        def packed_operand(w, a, t):
            codes = w_words[w][:, a, t * P // 2 : (t + 1) * P // 2]
            plane = w_scales[:, w, a, t * P // 4 : (t + 1) * P // 4]
            return codes.bitcast(FP4X4), plane.bitcast(U8)

        def wc_operand(a, t):
            return wc_codes[t][:, a, :].bitcast(FP8X4), wc_scales[t][:, a, :]

        def accumulate(acc, operand_pairs):
            for i, ((lhs, lhs_scale), (rhs, rhs_scale)) in enumerate(operand_pairs):
                nc.tensor.matmul_mx(
                    out=acc[:],
                    lhsT=lhs,
                    lhsT_scale=lhs_scale,
                    rhs=rhs,
                    rhs_scale=rhs_scale,
                    start=(i == 0),
                    stop=(i == len(operand_pairs) - 1),
                )

        messages, values = {}, {}

        def message(u):
            t, half = UNITS[u]
            za = psum.tile([P, EDGES], F32, name="za")
            ms = psum.tile([P, EDGES], F32, name="ms")
            accumulate(
                za,
                [
                    (packed_operand(w, a, t), table_operand(half, side, a))
                    for w, side in ((WA, TGT), (WB, SRC))
                    for a in range(PASSES)
                ],
            )
            accumulate(ms, [(wc_operand(a, t), table_operand(half, SRC, a)) for a in range(PASSES)])
            tanh = ring.tile([P, EDGES], F32, name="tanh")
            nc.scalar.activation(tanh[:], za[:], ACT.Tanh, bias=zero[:], scale=0.5)
            gated = ring.tile([P, EDGES], F32, name="gated")
            if u in GATE_ON_VECTOR:
                nc.vector.scalar_tensor_tensor(gated[:], tanh[:], 1.0, ms[:], ALU.add, ALU.mult)
            else:
                gate = ring.tile([P, EDGES], F32, name="gate")
                nc.scalar.activation(gate[:], tanh[:], ACT.Identity, bias=1.0)
                ms_copy = ring.tile([P, EDGES], F32, name="ms_copy")
                nc.scalar.copy(ms_copy[:], ms[:])
                nc.gpsimd.tensor_tensor(gated[:], gate[:], ms_copy[:], ALU.mult)
            messages[u] = gated

        def weight_of(u):
            half = UNITS[u][1]
            return edge_w[:, half * EDGES : (half + 1) * EDGES]

        def value(u):
            t, half = UNITS[u]
            ow = psum.tile([P, EDGES], F32, name="ow", bufs=2)
            accumulate(ow, [(packed_operand(WO, a, t), table_operand(half, TGT, a)) for a in range(PASSES)])
            twice = ring.tile([P, EDGES], F32, name="twice")
            if u in SUM_ON_VECTOR:
                nc.vector.scalar_tensor_tensor(twice[:], ow[:], 2.0, messages[u][:], ALU.mult, ALU.add)
            else:
                ow_twice = ring.tile([P, EDGES], F32, name="ow_twice")
                nc.scalar.activation(ow_twice[:], ow[:], ACT.Copy, scale=2.0)
                nc.gpsimd.tensor_tensor(twice[:], messages[u][:], ow_twice[:], ALU.add)
            silu = ring.tile([P, EDGES], F32, name="silu")
            nc.scalar.activation(silu[:], twice[:], ACT.Silu, bias=bias[:, t : t + 1], scale=0.5)
            if u in WEIGHT_IN_SCATTER:
                values[u] = silu
            else:
                weighted = ring.tile([P, EDGES], F32, name="weighted", bufs=len(UNITS) - len(WEIGHT_IN_SCATTER))
                engine = nc.vector if u in WEIGHT_ON_VECTOR else nc.gpsimd
                engine.tensor_tensor(weighted[:], silu[:], weight_of(u), ALU.mult)
                values[u] = weighted

        def scatter(u):
            t, half = UNITS[u]
            window = windows[t % WINDOWS]
            places = window[:].indirect(list_half(TGT, half))
            if u in WEIGHT_IN_SCATTER:
                nc.vector.tensor_tensor(places, values[u][:], weight_of(u), ALU.mult)
            else:
                nc.vector.tensor_copy(places, values[u][:])
            if all(later[0] != t for later in UNITS[u + 1 :]):
                nc.sync.dma_start(out[t * P : (t + 1) * P, :], window[:])

        nc.sync.dma_start(lists[TGT][:], offs2)
        nc.sync.dma_start(lists[SRC][:], offs)
        for q in range(QUADS):
            nc.sync.dma_start(scales[32 * q : 32 * q + 8, :], tab_scales[:, 4 * q : 4 * q + 4, :].bitcast(I32))
        nc.sync.dma_start(words[:], tab_words[0].rearrange("p t b -> p (t b)").bitcast(I32))
        load_scale_rows(WA, wa_scales)
        load_packed(WA, wa_words)
        load_wc(0, 1)
        load_packed(WO, wo_words)
        nc.sync.dma_start(edge_w[:], wgo)
        load_wc(1, 0)
        gather_scales()
        load_scale_rows(WB, wb_scales)
        load_wc(0, 0)
        load_packed(WB, wb_words)
        load_scale_rows(WO, wo_scales)
        load_wc(1, 1)
        with nc.allow_non_contiguous_dma("one bias value for each partition and channel tile"):
            nc.sync.dma_start(bias[:], b.rearrange("(t p) -> p t", p=P))

        first_pairs = {side: gather_words(0, side, "pairs%d" % side) for side in (TGT, SRC)}
        for side in (TGT, SRC):
            part_words(0, side, first_pairs[side])
        for t in range(TILES // 2):
            interleave_wc(t)
            quantize_wc(t)
        part_words(1, SRC, gather_words(1, SRC, "pairs%d" % TGT))
        part_words(1, TGT, gather_words(1, TGT, "wc_raw0"))
        for u in BATCHES[0]:
            message(u)
        second_half = range(TILES - 1, TILES // 2 - 1, -1)
        for t in second_half:
            interleave_wc(t)
        for u in BATCHES[0]:
            value(u)
        for t in second_half:
            quantize_wc(t)
        for batch in BATCHES[1:]:
            for u in batch:
                message(u)
            for u in batch:
                value(u)
        for u in range(len(UNITS)):
            scatter(u)
